import numpy as np
import ml_dtypes


def mxq(x, axis, fmt="e4m3"):
    dtype, down = {"e4m3": (ml_dtypes.float8_e4m3fn, 7), "e5m2": (ml_dtypes.float8_e5m2, 14)}[fmt]
    v = np.moveaxis(np.asarray(x, np.float32).astype(ml_dtypes.bfloat16).astype(np.float64), axis, -1)
    blocks = v.reshape(v.shape[:-1] + (-1, 32))
    amax = np.abs(blocks).max(-1, keepdims=True)
    byte = np.maximum(np.where(amax > 0, np.frexp(amax)[1] - 1 + 127, 0) - down, 1)
    scale = np.exp2(byte - 127.0)
    codes = (blocks / scale).astype(np.float32).astype(dtype).astype(np.float64)
    return np.moveaxis((codes * scale).reshape(v.shape), -1, axis)


WIDE = False


def mx_kscale(k):
    if not WIDE:
        return np.ones(k)
    levels = np.array([30, -30])
    if k % 512:
        return np.exp2(np.random.permutation(np.resize(levels, k // 32))).repeat(32)
    a = np.empty((k // 512, 16))
    for p in range(k // 512):
        a[p, :8] = np.random.permutation(np.resize(levels, 8))
        for g in range(8):
            far = levels[np.abs(levels - a[p, g]) >= 10]
            a[p, g + 8] = far[np.random.randint(len(far))]
    return np.exp2(a.ravel()).repeat(32)


def f64(x):
    return np.asarray(x).astype(np.float64)


def striped(idx):
    return np.tile(np.asarray(idx).reshape(-1, 16).T, (8, 1)).astype(np.uint16)


def unstriped(offs):
    return offs[:16].T.reshape(-1).astype(np.int64)


E2M1 = np.array([0.0, 0.5, 1.0, 1.5, 2.0, 3.0, 4.0, 6.0, -0.0, -0.5, -1.0, -1.5, -2.0, -3.0, -4.0, -6.0])


def pack_weight(w, fmt):
    k, n = w.shape
    w = f64(np.asarray(w, np.float32).astype(ml_dtypes.bfloat16)).reshape(k // 32, 32, n)
    amax = np.abs(w).max(1)
    if fmt in ("e4m3", "e5m2"):
        byte = np.frexp(amax)[1] - 1 + 127 - (7 if fmt == "e4m3" else 14)
    else:
        mant, ex = np.frexp(amax / 6.0)
        byte = np.where(mant > 0.5, ex, ex - 1) + 127
    byte = np.clip(np.where(amax > 0, byte, 1), 1, 254)
    scaled = (w * np.exp2(127.0 - byte)[:, None, :]).reshape(k, n).astype(np.float32)
    by_word = np.ascontiguousarray(scaled.reshape(k // 512, 128, 4, n).transpose(0, 1, 3, 2))
    if fmt in ("e4m3", "e5m2"):
        words = by_word.astype(ml_dtypes.float8_e4m3fn if fmt == "e4m3" else ml_dtypes.float8_e5m2).view(np.uint8)
    else:
        c = by_word.astype(ml_dtypes.float4_e2m1fn).view(np.uint8) & 0xF
        words = (c[..., 0::2] | (c[..., 1::2] << 4)).reshape(k // 512, 128, 2 * n)
    return np.ascontiguousarray(words), np.ascontiguousarray(byte.astype(np.uint8).reshape(k // 512, 16, n))


def unpack_weight(words, scales, fmt):
    g, _, n = scales.shape
    words = np.ascontiguousarray(words).reshape(g, 128, n, -1)
    if fmt in ("e4m3", "e5m2"):
        vals = words.view(ml_dtypes.float8_e4m3fn if fmt == "e4m3" else ml_dtypes.float8_e5m2).astype(np.float64)
    else:
        nib = np.empty((g, 128, n, 4), np.uint8)
        nib[..., 0::2] = words & 0xF
        nib[..., 1::2] = words >> 4
        vals = E2M1[nib]
    vals = vals * np.repeat(np.exp2(scales.astype(np.float64) - 127.0), 8, axis=1)[..., None]
    return vals.transpose(0, 1, 3, 2).reshape(g * 512, n)


def sigmoid(v):
    return 1.0 / (1.0 + np.exp(-v))


def sgn(shape):
    return np.random.uniform(0.5, 2.0, shape) * np.where(np.random.standard_normal(shape) < 0, -1.0, 1.0)


K, T, J, R, O, N = 512, 1024, 256, 512, 128, 256


def setup_inputs():
    n = np.random.standard_normal
    idx = np.random.permutation(T)[:J]
    idx2 = np.random.permutation(J)[:J]
    idx3 = np.random.permutation(J)[:O]
    fk = mx_kscale(K)
    fr = mx_kscale(R)
    fr = fr / fr.max()
    xtp = pack_weight(n((K, T)) / fk[:, None], "e2m1")
    wp = pack_weight(n((K, R)) * 1 / np.sqrt(K) * fk[:, None], "e4m3")
    w2p = pack_weight(n((K, R)) * 1 / np.sqrt(K) * fk[:, None], "e5m2")
    wbp = pack_weight(n((R, N)) * 1 / np.sqrt(R) / fr[:, None], "e4m3")
    return {
        "xt_words": xtp[0],
        "xt_scales": xtp[1],
        "w_words": wp[0],
        "w_scales": wp[1],
        "w2_words": w2p[0],
        "w2_scales": w2p[1],
        "sg": (0.3 * sgn((R, 1))).astype(np.float32),
        "lo": (np.random.uniform(-2.6, -1.2, (R, 1)) + np.log(fr)[:, None]).astype(np.float32),
        "wb_words": wbp[0],
        "wb_scales": wbp[1],
        "offs": striped(idx),
        "offs2": striped(idx2),
        "offs3": striped(idx3),
    }


def reference(xt_words, xt_scales, w_words, w_scales, w2_words, w2_scales, sg, lo, wb_words, wb_scales, offs, offs2, offs3):
    idx = unstriped(offs)
    idx2 = unstriped(offs2)
    idx3 = unstriped(offs3)
    xtu = unpack_weight(xt_words, xt_scales, "e2m1")
    wu = unpack_weight(w_words, w_scales, "e4m3")
    w2u = unpack_weight(w2_words, w2_scales, "e5m2")
    wbu = unpack_weight(wb_words, wb_scales, "e4m3")
    xtidxg = xtu[:, idx]
    a = wu.T @ xtidxg
    b = w2u.T @ xtidxg
    g1 = np.maximum(a, b[:, idx2])
    hid = sigmoid(g1[:, idx3] * f64(sg) + f64(lo))
    hidq = mxq(hid, 0, "e4m3")
    p = wbu.T @ hidq
    return p

@@ -1,0 +1,174 @@
+from contextlib import ExitStack
+
+import concourse.mybir as mybir
+
+K, T, J, R, O, N = 512, 1024, 256, 512, 128, 256
+FLOPS = 2 * K * R * J * 2 + 2 * R * N * O
+
+F32 = mybir.dt.float32
+BF16 = mybir.dt.bfloat16
+I32 = mybir.dt.int32
+U32 = mybir.dt.uint32
+U16 = mybir.dt.uint16
+U8 = mybir.dt.uint8
+E4M3 = mybir.dt.float8_e4m3fn_x4
+E5M2 = mybir.dt.float8_e5m2_x4
+E2M1 = mybir.dt.float4_e2m1fn_x4
+ACT = mybir.ActivationFunctionType
+ALU = mybir.AluOpType
+
+P = 128
+PACK = 4
+
+
+def tile_list_partnersig_kernel(tc, xt_words, xt_scales, w_words, w_scales, w2_words, w2_scales, sg, lo,
+                                    wb_words, wb_scales, offs, offs2, offs3, out):
+    nc = tc.nc
+    with ExitStack() as ctx:
+        sb = ctx.enter_context(tc.tile_pool(name="sb", bufs=1))
+        reuse = ctx.enter_context(tc.tile_pool(name="reuse", bufs=1))
+        ps = ctx.enter_context(tc.psum_pool(name="ps", bufs=1))
+
+        def tile(name, cols, dtype):
+            return sb.tile([P, cols], dtype, name=name, align_bytes=64)
+
+        def placed(name, cols, dtype, offset):
+            return reuse.tile([P, cols], dtype, name=name, align_bytes=64, offset=offset)
+
+        list1 = sb.tile([P, J // 16], U16, name="list1")
+        list2 = sb.tile([P, J // 16], U16, name="list2")
+        list3 = sb.tile([P, O // 16], U16, name="list3")
+        x_words = tile("x_words", T, U16)
+        x_plane = placed("x_plane", T, U8, 0)
+        w_raw = tile("w_raw", R, U32)
+        w2_raw = tile("w2_raw", R, U32)
+        w_plane_raw = placed("w_plane_raw", R, U8, 4096)
+        w2_plane_raw = tile("w2_plane_raw", R, U8)
+        w2_rows = tile("w2_rows", 4 * R, U8)
+        wb_codes = tile("wb_codes", N, U32)
+        wb_plane = tile("wb_plane", N, U8)
+        slope = tile("slope", PACK, F32)
+        shift = tile("shift", PACK, F32)
+
+        nc.vector.memset(x_plane[:].bitcast(I32), 0)
+        nc.vector.memset(w2_plane_raw[:].bitcast(I32), 0)
+        nc.vector.memset(w_plane_raw[:].bitcast(I32), 0)
+        nc.vector.memset(wb_plane[:].bitcast(I32), 0)
+
+        def load_words(queue, dst, src):
+            queue.dma_start(dst[:].bitcast(I32), src[0].rearrange("p n t -> p (n t)").bitcast(I32))
+
+        def load_plane(queue, dst, src, q):
+            queue.dma_start(dst[32 * q : 32 * q + 4, :].bitcast(I32), src[0, 4 * q : 4 * q + 4, :].bitcast(I32))
+
+        nc.sync.dma_start(x_words[:].bitcast(I32), xt_words[0].bitcast(I32))
+        nc.scalar.dma_start(w2_rows[0:4, :].bitcast(I32).rearrange("r (q c) -> r q c", q=4),
+                            w2_scales[0].bitcast(I32).rearrange("(q r) c -> r q c", q=4))
+        nc.sync.dma_start(list1[:], offs)
+        for q in range(4):
+            load_plane(nc.sync if q < 2 else nc.scalar, x_plane, xt_scales, q)
+        load_words(nc.sync, w2_raw, w2_words)
+        load_words(nc.gpsimd, w_raw, w_words)
+        nc.sync.dma_start(list2[:], offs2)
+        for q in range(4):
+            load_plane(nc.sync, w_plane_raw, w_scales, q)
+        nc.sync.dma_start(list3[:], offs3)
+        nc.sync.dma_start(slope[:], sg.rearrange("(p t) o -> p (t o)", t=PACK))
+        nc.sync.dma_start(shift[:], lo.rearrange("(p t) o -> p (t o)", t=PACK))
+        load_words(nc.sync, wb_codes, wb_words)
+        for q in range(4):
+            load_plane(nc.sync, wb_plane, wb_scales, q)
+
+        w_codes = placed("w_codes", R, U32, 512)
+        w2_codes = tile("w2_codes", R, U32)
+        w_plane = tile("w_plane", R, U8)
+        w2_plane_first = tile("w2_plane_first", P, U8)
+        w2_plane_rest = placed("w2_plane_rest", R - P, U8, 0)
+        w2_planes = [w2_plane_first[:]] + [w2_plane_rest[:, t * P : (t + 1) * P] for t in range(PACK - 1)]
+        w_planes = [w_plane[:, t * P : (t + 1) * P] for t in range(PACK)]
+
+        def by_slot(raw):
+            return raw[:].rearrange("p (m t) -> p t m", t=PACK)
+
+        for q in range(4):
+            nc.vector.tensor_copy(w2_plane_raw[32 * q : 32 * q + 4, :].bitcast(I32), w2_rows[0:4, q * R : (q + 1) * R].bitcast(I32))
+        nc.vector.tensor_copy(w2_plane_first[:], by_slot(w2_plane_raw)[:, 0, :])
+        nc.scalar.copy(w2_codes[:].rearrange("p (t m) -> p m t", t=PACK), w2_raw[:].rearrange("p (m t) -> p m t", t=PACK))
+
+        xg_words = tile("xg_words", J, U16)
+        xg_plane = tile("xg_plane", J, U8)
+        nc.vector.tensor_copy(xg_words[:], x_words[:].indirect(list1[:]))
+        nc.vector.tensor_copy(xg_plane[:], x_plane[:].indirect(list1[:]))
+        nc.vector.tensor_copy(w2_plane_rest[:].rearrange("p (t m) -> p t m", m=P), by_slot(w2_plane_raw)[:, 1:, :])
+        nc.vector.tensor_copy(w_codes[:].bitcast(I32).rearrange("p (t m) -> p m t", t=PACK),
+                              w_raw[:].bitcast(I32).rearrange("p (m t) -> p m t", t=PACK))
+
+        def first_stage(name, codes, planes, fmt, t):
+            acc = ps.tile([P, J], F32, name=name, tag=name)
+            nc.tensor.matmul_mx(acc[:], lhsT=codes[:, t * P : (t + 1) * P].bitcast(fmt), lhsT_scale=planes[t],
+                                rhs=xg_words[:].bitcast(E2M1), rhs_scale=xg_plane[:], start=True, stop=True)
+            return acc
+
+        b_ps = [first_stage("b_ps%d" % t, w2_codes, w2_planes, E5M2, t) for t in range(PACK)]
+
+        b_sb = [tile("b_sb%d" % t, J, F32) for t in range(PACK)]
+        partner = [placed("partner%d" % t, J, F32, 4096 - 256) if t == 1 else tile("partner%d" % t, J, F32) for t in range(PACK)]
+        kept = [tile("kept%d" % t, J, F32) for t in range(PACK)]
+        hid = tile("hid", PACK * O, BF16)
+        half = J // 2
+        a_ps = {}
+
+        def evac(eng, t):
+            if eng == "v":
+                nc.vector.tensor_copy(b_sb[t][:], b_ps[t][:])
+            else:
+                nc.scalar.copy(b_sb[t][:], b_ps[t][:])
+
+        def look_up(eng, t, h):
+            dst = partner[t][:, h * half : (h + 1) * half]
+            src = b_sb[t][:].indirect(list2[:, h * half // 16 : (h + 1) * half // 16])
+            if eng == "v":
+                nc.vector.tensor_copy(dst, src)
+            else:
+                nc.scalar.activation(dst, src, ACT.Copy)
+
+        def keep(t):
+            nc.vector.tensor_tensor(kept[t][:], a_ps[t][:], partner[t][:], ALU.max)
+
+        def fetch(t):
+            nc.scalar.activation(hid[:, t : PACK * O : PACK], kept[t][:].indirect(list3[:]), ACT.Sigmoid,
+                                 bias=shift[:, t : t + 1], scale=slope[:, t : t + 1])
+
+        for t in range(PACK):
+            evac("s", t)
+        look_up("v", 0, 0)
+        look_up("v", 0, 1)
+        nc.vector.tensor_copy(w_plane[:].rearrange("p (t m) -> p t m", m=P), by_slot(w_plane_raw))
+        for t in range(PACK):
+            a_ps[t] = first_stage("a_ps%d" % t, w_codes, w_planes, E4M3, t)
+        look_up("v", 1, 0)
+        look_up("v", 1, 1)
+        look_up("s", 2, 0)
+        look_up("s", 2, 1)
+        look_up("s", 3, 0)
+        look_up("s", 3, 1)
+        for t in range(PACK):
+            keep(t)
+            fetch(t)
+
+        hid_codes = tile("hid_codes", O, U32)
+        hid_plane = tile("hid_plane", O, U8)
+        nc.vector.quantize_mx(out=hid_codes[:].bitcast(E4M3), scales=hid_plane[:], in_=hid[:])
+
+        for h in range(N // P):
+            cols = slice(h * P, (h + 1) * P)
+            acc = ps.tile([P, O], F32, name="out_ps%d" % h, tag="b_ps%d" % h)
+            nc.tensor.matmul_mx(acc[:], lhsT=wb_codes[:, cols].bitcast(E4M3), lhsT_scale=wb_plane[:, cols],
+                                rhs=hid_codes[:].bitcast(E4M3), rhs_scale=hid_plane[:], start=True, stop=True)
+            res = tile("res%d" % h, O, F32)
+            if h == 0:
+                nc.vector.tensor_copy(res[:], acc[:])
+                nc.sync.dma_start(out[cols, :], res[:])
+            else:
+                nc.scalar.copy(res[:], acc[:])
+                nc.scalar.dma_start(out[cols, :], res[:])

@@ -79,6 +79,11 @@ def tile_list_partnersig_kernel(tc, xt_words, xt_scales, w_words, w_scales, w2_w
         for q in range(4):
             load_plane(nc.sync, wb_plane, wb_scales, q)
 
+        warm_in = tile("warm_in", 1, F32)
+        warm_out = tile("warm_out", 1, F32)
+        nc.vector.memset(warm_in[:], 0.0)
+        nc.scalar.activation(warm_out[:], warm_in[:], ACT.Sigmoid)
+
         w_codes = placed("w_codes", R, U32, 512)
         w2_codes = tile("w2_codes", R, U32)
         w_plane = tile("w_plane", R, U8)

@@ -39,10 +39,10 @@ def tile_list_partnersig_kernel(tc, xt_words, xt_scales, w_words, w_scales, w2_w
         list2 = sb.tile([P, J // 16], U16, name="list2")
         list3 = sb.tile([P, O // 16], U16, name="list3")
         x_words = tile("x_words", T, U16)
-        x_plane = placed("x_plane", T, U8, 0)
+        x_plane = tile("x_plane", T, U8)
         w_raw = tile("w_raw", R, U32)
-        w2_raw = tile("w2_raw", R, U32)
-        w_plane_raw = placed("w_plane_raw", R, U8, 4096)
+        w2_raw = placed("w2_raw", R, U32, 8192)
+        w_plane_raw = tile("w_plane_raw", R, U8)
         w2_plane_raw = tile("w2_plane_raw", R, U8)
         w2_rows = tile("w2_rows", 4 * R, U8)
         wb_codes = tile("wb_codes", N, U32)
@@ -52,8 +52,8 @@ def tile_list_partnersig_kernel(tc, xt_words, xt_scales, w_words, w_scales, w2_w
 
         nc.vector.memset(x_plane[:].bitcast(I32), 0)
         nc.vector.memset(w2_plane_raw[:].bitcast(I32), 0)
-        nc.vector.memset(w_plane_raw[:].bitcast(I32), 0)
-        nc.vector.memset(wb_plane[:].bitcast(I32), 0)
+        nc.gpsimd.memset(w_plane_raw[:].bitcast(I32), 0)
+        nc.gpsimd.memset(wb_plane[:].bitcast(I32), 0)
 
         def load_words(queue, dst, src):
             queue.dma_start(dst[:].bitcast(I32), src[0].rearrange("p n t -> p (n t)").bitcast(I32))
@@ -61,18 +61,18 @@ def tile_list_partnersig_kernel(tc, xt_words, xt_scales, w_words, w_scales, w2_w
         def load_plane(queue, dst, src, q):
             queue.dma_start(dst[32 * q : 32 * q + 4, :].bitcast(I32), src[0, 4 * q : 4 * q + 4, :].bitcast(I32))
 
+        nc.sync.dma_start(list1[:], offs)
         nc.sync.dma_start(x_words[:].bitcast(I32), xt_words[0].bitcast(I32))
         nc.scalar.dma_start(w2_rows[0:4, :].bitcast(I32).rearrange("r (q c) -> r q c", q=4),
                             w2_scales[0].bitcast(I32).rearrange("(q r) c -> r q c", q=4))
-        nc.sync.dma_start(list1[:], offs)
         for q in range(4):
             load_plane(nc.sync if q < 2 else nc.scalar, x_plane, xt_scales, q)
         load_words(nc.sync, w2_raw, w2_words)
         load_words(nc.gpsimd, w_raw, w_words)
-        nc.sync.dma_start(list2[:], offs2)
         for q in range(4):
             load_plane(nc.sync, w_plane_raw, w_scales, q)
         nc.sync.dma_start(list3[:], offs3)
+        nc.sync.dma_start(list2[:], offs2)
         nc.sync.dma_start(slope[:], sg.rearrange("(p t) o -> p (t o)", t=PACK))
         nc.sync.dma_start(shift[:], lo.rearrange("(p t) o -> p (t o)", t=PACK))
         load_words(nc.sync, wb_codes, wb_words)
@@ -84,12 +84,13 @@ def tile_list_partnersig_kernel(tc, xt_words, xt_scales, w_words, w_scales, w2_w
         nc.vector.memset(warm_in[:], 0.0)
         nc.scalar.activation(warm_out[:], warm_in[:], ACT.Sigmoid)
 
-        w_codes = placed("w_codes", R, U32, 512)
-        w2_codes = tile("w2_codes", R, U32)
+        w_codes = placed("w_codes", R, U32, 8192)
+        w2_codes = [tile("w2_codes%d" % u, 2 * P, U32) for u in range(2)]
+        w2_slots = [w2_codes[t // 2][:, (t % 2) * P : (t % 2 + 1) * P] for t in range(PACK)]
+        w_slots = [w_codes[:, t * P : (t + 1) * P] for t in range(PACK)]
         w_plane = tile("w_plane", R, U8)
-        w2_plane_first = tile("w2_plane_first", P, U8)
-        w2_plane_rest = placed("w2_plane_rest", R - P, U8, 0)
-        w2_planes = [w2_plane_first[:]] + [w2_plane_rest[:, t * P : (t + 1) * P] for t in range(PACK - 1)]
+        w2_plane = [tile("w2_plane%d" % u, 2 * P, U8) for u in range(2)]
+        w2_planes = [w2_plane[t // 2][:, (t % 2) * P : (t % 2 + 1) * P] for t in range(PACK)]
         w_planes = [w_plane[:, t * P : (t + 1) * P] for t in range(PACK)]
 
         def by_slot(raw):
@@ -97,27 +98,34 @@ def tile_list_partnersig_kernel(tc, xt_words, xt_scales, w_words, w_scales, w2_w
 
         for q in range(4):
             nc.vector.tensor_copy(w2_plane_raw[32 * q : 32 * q + 4, :].bitcast(I32), w2_rows[0:4, q * R : (q + 1) * R].bitcast(I32))
-        nc.vector.tensor_copy(w2_plane_first[:], by_slot(w2_plane_raw)[:, 0, :])
-        nc.scalar.copy(w2_codes[:].rearrange("p (t m) -> p m t", t=PACK), w2_raw[:].rearrange("p (m t) -> p m t", t=PACK))
+        for u in range(2):
+            nc.gpsimd.tensor_copy(w2_plane[u][:].rearrange("p (t m) -> p t m", m=P), by_slot(w2_plane_raw)[:, 2 * u : 2 * u + 2, :])
+        for u in range(2):
+            nc.scalar.copy(w2_codes[u][:].rearrange("p (t m) -> p m t", t=2),
+                           w2_raw[:].rearrange("p (m t) -> p m t", t=PACK)[:, :, 2 * u : 2 * u + 2])
 
         xg_words = tile("xg_words", J, U16)
         xg_plane = tile("xg_plane", J, U8)
         nc.vector.tensor_copy(xg_words[:], x_words[:].indirect(list1[:]))
-        nc.vector.tensor_copy(xg_plane[:], x_plane[:].indirect(list1[:]))
-        nc.vector.tensor_copy(w2_plane_rest[:].rearrange("p (t m) -> p t m", m=P), by_slot(w2_plane_raw)[:, 1:, :])
-        nc.vector.tensor_copy(w_codes[:].bitcast(I32).rearrange("p (t m) -> p m t", t=PACK),
-                              w_raw[:].bitcast(I32).rearrange("p (m t) -> p m t", t=PACK))
+        for h in range(2):
+            nc.vector.tensor_copy(xg_plane[:, h * P : (h + 1) * P], x_plane[:].indirect(list1[:, 8 * h : 8 * h + 8]))
+        nc.scalar.copy(w_codes[:].rearrange("p (t m) -> p m t", t=PACK), w_raw[:].rearrange("p (m t) -> p m t", t=PACK))
+        nc.gpsimd.tensor_copy(w_plane[:].rearrange("p (t m) -> p t m", m=P), by_slot(w_plane_raw))
 
         def first_stage(name, codes, planes, fmt, t):
             acc = ps.tile([P, J], F32, name=name, tag=name)
-            nc.tensor.matmul_mx(acc[:], lhsT=codes[:, t * P : (t + 1) * P].bitcast(fmt), lhsT_scale=planes[t],
+            nc.tensor.matmul_mx(acc[:], lhsT=codes[t].bitcast(fmt), lhsT_scale=planes[t],
                                 rhs=xg_words[:].bitcast(E2M1), rhs_scale=xg_plane[:], start=True, stop=True)
             return acc
 
-        b_ps = [first_stage("b_ps%d" % t, w2_codes, w2_planes, E5M2, t) for t in range(PACK)]
+        b_ps = [ps.tile([P, J], F32, name="b_ps%d" % t, tag="b_ps%d" % t) for t in range(PACK)]
+        for t, cols in ((0, slice(0, P)), (1, slice(0, P)), (0, slice(P, J)), (1, slice(P, J)), (2, slice(0, J)), (3, slice(0, J))):
+            nc.tensor.matmul_mx(b_ps[t][:, cols], lhsT=w2_slots[t].bitcast(E5M2), lhsT_scale=w2_planes[t],
+                                rhs=xg_words[:, cols].bitcast(E2M1), rhs_scale=xg_plane[:, cols], start=True, stop=True)
 
         b_sb = [tile("b_sb%d" % t, J, F32) for t in range(PACK)]
-        partner = [placed("partner%d" % t, J, F32, 4096 - 256) if t == 1 else tile("partner%d" % t, J, F32) for t in range(PACK)]
+        partner = [placed("partner0", J, F32, 0) if t == 0 else tile("partner%d" % t, J, F32) for t in range(PACK)]
+        late_half = placed("late_half", J // 2, F32, 0)
         kept = [tile("kept%d" % t, J, F32) for t in range(PACK)]
         hid = tile("hid", PACK * O, BF16)
         half = J // 2
@@ -130,7 +138,7 @@ def tile_list_partnersig_kernel(tc, xt_words, xt_scales, w_words, w_scales, w2_w
                 nc.scalar.copy(b_sb[t][:], b_ps[t][:])
 
         def look_up(eng, t, h):
-            dst = partner[t][:, h * half : (h + 1) * half]
+            dst = late_half[:] if (t, h) == (2, 1) else partner[t][:, h * half : (h + 1) * half]
             src = b_sb[t][:].indirect(list2[:, h * half // 16 : (h + 1) * half // 16])
             if eng == "v":
                 nc.vector.tensor_copy(dst, src)
@@ -138,27 +146,32 @@ def tile_list_partnersig_kernel(tc, xt_words, xt_scales, w_words, w_scales, w2_w
                 nc.scalar.activation(dst, src, ACT.Copy)
 
         def keep(t):
-            nc.vector.tensor_tensor(kept[t][:], a_ps[t][:], partner[t][:], ALU.max)
+            if t == 2:
+                nc.vector.tensor_tensor(kept[t][:, :half], a_ps[t][:, :half], partner[t][:, :half], ALU.max)
+                nc.vector.tensor_tensor(kept[t][:, half:], a_ps[t][:, half:], late_half[:], ALU.max)
+            else:
+                nc.vector.tensor_tensor(kept[t][:], a_ps[t][:], partner[t][:], ALU.max)
 
         def fetch(t):
             nc.scalar.activation(hid[:, t : PACK * O : PACK], kept[t][:].indirect(list3[:]), ACT.Sigmoid,
                                  bias=shift[:, t : t + 1], scale=slope[:, t : t + 1])
 
+        for t in (0, 1, 3, 2):
+            a_ps[t] = first_stage("a_ps%d" % t, w_slots, w_planes, E4M3, t)
         for t in range(PACK):
-            evac("s", t)
+            evac("s" if t % 2 else "v", t)
+        for t in (1, 3):
+            for h in range(2):
+                look_up("s", t, h)
         look_up("v", 0, 0)
         look_up("v", 0, 1)
-        nc.vector.tensor_copy(w_plane[:].rearrange("p (t m) -> p t m", m=P), by_slot(w_plane_raw))
-        for t in range(PACK):
-            a_ps[t] = first_stage("a_ps%d" % t, w_codes, w_planes, E4M3, t)
-        look_up("v", 1, 0)
-        look_up("v", 1, 1)
-        look_up("s", 2, 0)
-        look_up("s", 2, 1)
-        look_up("s", 3, 0)
-        look_up("s", 3, 1)
-        for t in range(PACK):
-            keep(t)
+        look_up("v", 2, 0)
+        keep(0)
+        keep(1)
+        look_up("v", 2, 1)
+        keep(3)
+        keep(2)
+        for t in (0, 1, 3, 2):
             fetch(t)
 
         hid_codes = tile("hid_codes", O, U32)

from contextlib import ExitStack

import concourse.mybir as mybir

K, T, J, R, O, N = 512, 1024, 256, 512, 128, 256
FLOPS = 2 * K * R * J * 2 + 2 * R * N * O

F32 = mybir.dt.float32
BF16 = mybir.dt.bfloat16
I32 = mybir.dt.int32
U32 = mybir.dt.uint32
U16 = mybir.dt.uint16
U8 = mybir.dt.uint8
E4M3 = mybir.dt.float8_e4m3fn_x4
E5M2 = mybir.dt.float8_e5m2_x4
E2M1 = mybir.dt.float4_e2m1fn_x4
ACT = mybir.ActivationFunctionType
ALU = mybir.AluOpType

P = 128
PACK = 4


def tile_list_partnersig_kernel(tc, xt_words, xt_scales, w_words, w_scales, w2_words, w2_scales, sg, lo,
                                    wb_words, wb_scales, offs, offs2, offs3, out):
    nc = tc.nc
    with ExitStack() as ctx:
        sb = ctx.enter_context(tc.tile_pool(name="sb", bufs=1))
        reuse = ctx.enter_context(tc.tile_pool(name="reuse", bufs=1))
        ps = ctx.enter_context(tc.psum_pool(name="ps", bufs=1))

        def tile(name, cols, dtype):
            return sb.tile([P, cols], dtype, name=name, align_bytes=64)

        def placed(name, cols, dtype, offset):
            return reuse.tile([P, cols], dtype, name=name, align_bytes=64, offset=offset)

        list1 = sb.tile([P, J // 16], U16, name="list1")
        list2 = sb.tile([P, J // 16], U16, name="list2")
        list3 = sb.tile([P, O // 16], U16, name="list3")
        x_words = tile("x_words", T, U16)
        x_plane = tile("x_plane", T, U8)
        w_raw = tile("w_raw", R, U32)
        w2_raw = placed("w2_raw", R, U32, 8192)
        w_plane_raw = tile("w_plane_raw", R, U8)
        w2_plane_raw = tile("w2_plane_raw", R, U8)
        w2_rows = tile("w2_rows", 4 * R, U8)
        wb_codes = tile("wb_codes", N, U32)
        wb_plane = tile("wb_plane", N, U8)
        slope = tile("slope", PACK, F32)
        shift = tile("shift", PACK, F32)

        nc.vector.memset(x_plane[:].bitcast(I32), 0)
        nc.vector.memset(w2_plane_raw[:].bitcast(I32), 0)
        nc.gpsimd.memset(w_plane_raw[:].bitcast(I32), 0)
        nc.gpsimd.memset(wb_plane[:].bitcast(I32), 0)

        def load_words(queue, dst, src):
            queue.dma_start(dst[:].bitcast(I32), src[0].rearrange("p n t -> p (n t)").bitcast(I32))

        def load_plane(queue, dst, src, q):
            queue.dma_start(dst[32 * q : 32 * q + 4, :].bitcast(I32), src[0, 4 * q : 4 * q + 4, :].bitcast(I32))

        nc.sync.dma_start(list1[:], offs)
        nc.sync.dma_start(x_words[:].bitcast(I32), xt_words[0].bitcast(I32))
        nc.scalar.dma_start(w2_rows[0:4, :].bitcast(I32).rearrange("r (q c) -> r q c", q=4),
                            w2_scales[0].bitcast(I32).rearrange("(q r) c -> r q c", q=4))
        for q in range(4):
            load_plane(nc.sync if q < 2 else nc.scalar, x_plane, xt_scales, q)
        load_words(nc.sync, w2_raw, w2_words)
        load_words(nc.gpsimd, w_raw, w_words)
        for q in range(4):
            load_plane(nc.sync, w_plane_raw, w_scales, q)
        nc.sync.dma_start(list3[:], offs3)
        nc.sync.dma_start(list2[:], offs2)
        nc.sync.dma_start(slope[:], sg.rearrange("(p t) o -> p (t o)", t=PACK))
        nc.sync.dma_start(shift[:], lo.rearrange("(p t) o -> p (t o)", t=PACK))
        load_words(nc.sync, wb_codes, wb_words)
        for q in range(4):
            load_plane(nc.sync, wb_plane, wb_scales, q)

        warm_in = tile("warm_in", 1, F32)
        warm_out = tile("warm_out", 1, F32)
        nc.vector.memset(warm_in[:], 0.0)
        nc.scalar.activation(warm_out[:], warm_in[:], ACT.Sigmoid)

        w_codes = placed("w_codes", R, U32, 8192)
        w2_codes = [tile("w2_codes%d" % u, 2 * P, U32) for u in range(2)]
        w2_slots = [w2_codes[t // 2][:, (t % 2) * P : (t % 2 + 1) * P] for t in range(PACK)]
        w_slots = [w_codes[:, t * P : (t + 1) * P] for t in range(PACK)]
        w_plane = tile("w_plane", R, U8)
        w2_plane = [tile("w2_plane%d" % u, 2 * P, U8) for u in range(2)]
        w2_planes = [w2_plane[t // 2][:, (t % 2) * P : (t % 2 + 1) * P] for t in range(PACK)]
        w_planes = [w_plane[:, t * P : (t + 1) * P] for t in range(PACK)]

        def by_slot(raw):
            return raw[:].rearrange("p (m t) -> p t m", t=PACK)

        for q in range(4):
            nc.vector.tensor_copy(w2_plane_raw[32 * q : 32 * q + 4, :].bitcast(I32), w2_rows[0:4, q * R : (q + 1) * R].bitcast(I32))
        for u in range(2):
            nc.gpsimd.tensor_copy(w2_plane[u][:].rearrange("p (t m) -> p t m", m=P), by_slot(w2_plane_raw)[:, 2 * u : 2 * u + 2, :])
        for u in range(2):
            nc.scalar.copy(w2_codes[u][:].rearrange("p (t m) -> p m t", t=2),
                           w2_raw[:].rearrange("p (m t) -> p m t", t=PACK)[:, :, 2 * u : 2 * u + 2])

        xg_words = tile("xg_words", J, U16)
        xg_plane = tile("xg_plane", J, U8)
        nc.vector.tensor_copy(xg_words[:], x_words[:].indirect(list1[:]))
        for h in range(2):
            nc.vector.tensor_copy(xg_plane[:, h * P : (h + 1) * P], x_plane[:].indirect(list1[:, 8 * h : 8 * h + 8]))
        nc.scalar.copy(w_codes[:].rearrange("p (t m) -> p m t", t=PACK), w_raw[:].rearrange("p (m t) -> p m t", t=PACK))
        nc.gpsimd.tensor_copy(w_plane[:].rearrange("p (t m) -> p t m", m=P), by_slot(w_plane_raw))

        def first_stage(name, codes, planes, fmt, t):
            acc = ps.tile([P, J], F32, name=name, tag=name)
            nc.tensor.matmul_mx(acc[:], lhsT=codes[t].bitcast(fmt), lhsT_scale=planes[t],
                                rhs=xg_words[:].bitcast(E2M1), rhs_scale=xg_plane[:], start=True, stop=True)
            return acc

        b_ps = [ps.tile([P, J], F32, name="b_ps%d" % t, tag="b_ps%d" % t) for t in range(PACK)]
        for t, cols in ((0, slice(0, P)), (1, slice(0, P)), (0, slice(P, J)), (1, slice(P, J)), (2, slice(0, J)), (3, slice(0, J))):
            nc.tensor.matmul_mx(b_ps[t][:, cols], lhsT=w2_slots[t].bitcast(E5M2), lhsT_scale=w2_planes[t],
                                rhs=xg_words[:, cols].bitcast(E2M1), rhs_scale=xg_plane[:, cols], start=True, stop=True)

        b_sb = [tile("b_sb%d" % t, J, F32) for t in range(PACK)]
        partner = [placed("partner0", J, F32, 0) if t == 0 else tile("partner%d" % t, J, F32) for t in range(PACK)]
        late_half = placed("late_half", J // 2, F32, 0)
        kept = [tile("kept%d" % t, J, F32) for t in range(PACK)]
        hid = tile("hid", PACK * O, BF16)
        half = J // 2
        a_ps = {}

        def evac(eng, t):
            if eng == "v":
                nc.vector.tensor_copy(b_sb[t][:], b_ps[t][:])
            else:
                nc.scalar.copy(b_sb[t][:], b_ps[t][:])

        def look_up(eng, t, h):
            dst = late_half[:] if (t, h) == (2, 1) else partner[t][:, h * half : (h + 1) * half]
            src = b_sb[t][:].indirect(list2[:, h * half // 16 : (h + 1) * half // 16])
            if eng == "v":
                nc.vector.tensor_copy(dst, src)
            else:
                nc.scalar.activation(dst, src, ACT.Copy)

        def keep(t):
            if t == 2:
                nc.vector.tensor_tensor(kept[t][:, :half], a_ps[t][:, :half], partner[t][:, :half], ALU.max)
                nc.vector.tensor_tensor(kept[t][:, half:], a_ps[t][:, half:], late_half[:], ALU.max)
            else:
                nc.vector.tensor_tensor(kept[t][:], a_ps[t][:], partner[t][:], ALU.max)

        def fetch(t):
            nc.scalar.activation(hid[:, t : PACK * O : PACK], kept[t][:].indirect(list3[:]), ACT.Sigmoid,
                                 bias=shift[:, t : t + 1], scale=slope[:, t : t + 1])

        for t in (0, 1, 3, 2):
            a_ps[t] = first_stage("a_ps%d" % t, w_slots, w_planes, E4M3, t)
        for t in range(PACK):
            evac("s" if t % 2 else "v", t)
        for t in (1, 3):
            for h in range(2):
                look_up("s", t, h)
        look_up("v", 0, 0)
        look_up("v", 0, 1)
        look_up("v", 2, 0)
        keep(0)
        keep(1)
        look_up("v", 2, 1)
        keep(3)
        keep(2)
        for t in (0, 1, 3, 2):
            fetch(t)

        hid_codes = tile("hid_codes", O, U32)
        hid_plane = tile("hid_plane", O, U8)
        nc.vector.quantize_mx(out=hid_codes[:].bitcast(E4M3), scales=hid_plane[:], in_=hid[:])

        for h in range(N // P):
            cols = slice(h * P, (h + 1) * P)
            acc = ps.tile([P, O], F32, name="out_ps%d" % h, tag="b_ps%d" % h)
            nc.tensor.matmul_mx(acc[:], lhsT=wb_codes[:, cols].bitcast(E4M3), lhsT_scale=wb_plane[:, cols],
                                rhs=hid_codes[:].bitcast(E4M3), rhs_scale=hid_plane[:], start=True, stop=True)
            res = tile("res%d" % h, O, F32)
            if h == 0:
                nc.vector.tensor_copy(res[:], acc[:])
                nc.sync.dma_start(out[cols, :], res[:])
            else:
                nc.scalar.copy(res[:], acc[:])
                nc.scalar.dma_start(out[cols, :], res[:])
